import numpy as np
import ml_dtypes


def mxq(x, axis, fmt="e4m3"):
    dtype, down = {"e4m3": (ml_dtypes.float8_e4m3fn, 7), "e5m2": (ml_dtypes.float8_e5m2, 14)}[fmt]
    v = np.moveaxis(np.asarray(x, np.float32).astype(ml_dtypes.bfloat16).astype(np.float64), axis, -1)
    blocks = v.reshape(v.shape[:-1] + (-1, 32))
    amax = np.abs(blocks).max(-1, keepdims=True)
    byte = np.maximum(np.where(amax > 0, np.frexp(amax)[1] - 1 + 127, 0) - down, 1)
    scale = np.exp2(byte - 127.0)
    codes = (blocks / scale).astype(np.float32).astype(dtype).astype(np.float64)
    return np.moveaxis((codes * scale).reshape(v.shape), -1, axis)


WIDE = False


def mx_kscale(k):
    if not WIDE:
        return np.ones(k)
    levels = np.array([10, -10, 5, -5, 0])
    if k % 512:
        return np.exp2(np.random.permutation(np.resize(levels, k // 32))).repeat(32)
    a = np.empty((k // 512, 16))
    for p in range(k // 512):
        a[p, :8] = np.random.permutation(np.resize(levels, 8))
        for g in range(8):
            far = levels[np.abs(levels - a[p, g]) >= 10]
            a[p, g + 8] = far[np.random.randint(len(far))]
    return np.exp2(a.ravel()).repeat(32)


def f64(x):
    return np.asarray(x).astype(np.float64)


def striped(idx):
    return np.tile(idx.reshape(-1, 16).T, (8, 1)).astype(np.uint16)


def unstriped(offs):
    return offs[:16].T.reshape(-1).astype(np.int64)


def pack_weight(w):
    k, n = w.shape
    w = f64(np.asarray(w, np.float32).astype(ml_dtypes.bfloat16)).reshape(k // 32, 32, n)
    amax = np.abs(w).max(1)
    byte = np.clip(np.where(amax > 0, np.frexp(amax)[1] - 1 + 127 - 7, 1), 1, 254)
    scaled = (w * np.exp2(127.0 - byte)[:, None, :]).reshape(k, n).astype(np.float32)
    words = np.ascontiguousarray(scaled.reshape(k // 512, 128, 4, n).transpose(0, 1, 3, 2)).astype(ml_dtypes.float8_e4m3fn).view(np.uint8)
    return words, np.ascontiguousarray(byte.astype(np.uint8).reshape(k // 512, 16, n))


def unpack_weight(words, scales):
    g, p, n, _ = words.shape
    vals = np.ascontiguousarray(words).view(ml_dtypes.float8_e4m3fn).astype(np.float64) * np.repeat(np.exp2(scales.astype(np.float64) - 127.0), 8, axis=1)[..., None]
    return vals.transpose(0, 1, 3, 2).reshape(g * 512, n)


K, T, E, C, N = 1024, 1024, 8, 256, 256


def by_expert(wq, xq):
    return np.concatenate([wq[e].T @ xq[:, e * C:(e + 1) * C] for e in range(E)], axis=1)


def setup_inputs():
    n = np.random.standard_normal
    s = mx_kscale(K)[:, None]
    first = np.random.permutation(np.repeat(np.arange(E), T // E))
    second = (first + 1 + np.random.permutation(np.repeat(np.arange(E - 1), -(-T // (E - 1)))[:T])) % E
    while np.bincount(second, minlength=E).max() != T // E:
        load = np.bincount(second, minlength=E); hi, lo = int(load.argmax()), int(load.argmin())
        t = np.flatnonzero((second == hi) & (first != lo))[0]; second[t] = lo
    slot_token = np.empty(E * C, np.int64); pos = np.empty((2, T), np.int64); fill = np.zeros(E, np.int64)
    place = np.stack([np.random.permutation(C) for _ in range(E)])
    for r, deal in enumerate((first, second)):
        for t in np.random.permutation(T):
            e = deal[t]; j = e * C + place[e, fill[e]]; fill[e] += 1; slot_token[j] = t; pos[r, t] = j
    g = np.random.uniform(0.2, 0.8, T)
    packed = [pack_weight(m) for m in n((E, K, N)) / np.sqrt(K) / s[None]]
    return {
        "xT": (n((K, T)) * s).astype(np.float32),
        "w_words": np.stack([m[0] for m in packed]),
        "w_scales": np.stack([m[1] for m in packed]),
        "gate": np.stack([np.tile(g, (N, 1)), np.tile(1.0 - g, (N, 1))]).astype(np.float32),
        "offs": striped(slot_token),
        "pos1": striped(pos[0]),
        "pos2": striped(pos[1]),
    }


def reference(xT, w_words, w_scales, gate, offs, pos1, pos2):
    idx = unstriped(offs)
    xq = mxq(f64(xT)[:, idx], 0, "e4m3")
    w = np.stack([unpack_weight(w_words[e], w_scales[e]) for e in range(E)])
    y = by_expert(w, xq)
    return f64(gate[0]) * y[:, unstriped(pos1)] + f64(gate[1]) * y[:, unstriped(pos2)]

@@ -1,0 +1,172 @@
+from contextlib import ExitStack
+
+import concourse.mybir as mybir
+from concourse.masks import make_identity
+
+K, T, E, C, N = 1024, 1024, 8, 256, 256
+FLOPS = 2 * K * N * E * C
+
+F32 = mybir.dt.float32
+BF16 = mybir.dt.bfloat16
+I32 = mybir.dt.int32
+U32 = mybir.dt.uint32
+U16 = mybir.dt.uint16
+U8 = mybir.dt.uint8
+FP8X4 = mybir.dt.float8_e4m3fn_x4
+MULT = mybir.AluOpType.mult
+ADD = mybir.AluOpType.add
+
+P = 128
+PASSES = K // 512
+SLOTS = E * C
+CH = 512
+NCH = T // CH
+HALVES = N // P
+CHUNKS = (((0, 512, 336), (512, 768, 168), (768, 1024, 200)), ((0, 512, 0), (512, 1024, 176)))
+W0_CUTS = (0, 768, 1536, 2048)
+W1_CUTS = (0, 768, 1536, 1792, 2048)
+B_CUTS = {0: 768, 768: 1536, 1536: 2048}
+
+
+def tile_routed_moe_kernel(tc, xT, w_words, w_scales, gate, offs, pos1, pos2, out):
+    nc = tc.nc
+    with ExitStack() as ctx:
+        lists = ctx.enter_context(tc.tile_pool(name="lists", bufs=1))
+        keep = ctx.enter_context(tc.tile_pool(name="keep", bufs=1))
+        psum = ctx.enter_context(tc.psum_pool(name="psum", bufs=1))
+
+        offs_t = lists.tile([P, SLOTS // 16], U16, name="offs_t")
+        pos1_t = lists.tile([P, T // 16], U16, name="pos1_t")
+        pos2_t = lists.tile([P, T // 16], U16, name="pos2_t")
+
+        xv = xT.rearrange("(a p t) n -> a p t n", p=P, t=4)
+        raw = {}
+        for a in range(PASSES):
+            for lo, hi, vshare in CHUNKS[a]:
+                raw[a, lo] = keep.tile([P, 4, hi - lo], F32, name="raw%d_%d" % (a, lo))
+                nc.sync.dma_start(out=raw[a, lo][:], in_=xv[a, :, :, lo:hi])
+                if a == 0 and lo == 0:
+                    nc.sync.dma_start(offs_t[:], offs)
+
+        ws = keep.tile([P, E * PASSES, N], U8, name="ws", align_bytes=64)
+        nc.vector.memset(ws[:].rearrange("p g n -> p (g n)").bitcast(I32), 0)
+        for q in range(4):
+            nc.sync.dma_start(
+                out=ws[32 * q:32 * q + 4, :, :].bitcast(I32),
+                in_=w_scales[:, :, 4 * q:4 * q + 4, :].rearrange("e a r n -> r (e a) n").bitcast(I32),
+            )
+        wv = w_words.rearrange("e a p n r -> p (e a) (n r)").bitcast(I32)
+        ww = []
+        for i in range(E // 2):
+            wt = keep.tile([P, 2 * PASSES, N], I32, name="ww%d" % i, align_bytes=64)
+            nc.sync.dma_start(out=wt[:], in_=wv[:, 2 * PASSES * i:2 * PASSES * (i + 1), :])
+            ww.append(wt)
+        nc.sync.dma_start(pos1_t[:], pos1)
+        nc.sync.dma_start(pos2_t[:], pos2)
+        gt = {}
+        for h in range(HALVES):
+            for r in range(2):
+                gt[r, h] = keep.tile([P, T], F32, name="gate%d%d" % (r, h))
+                nc.sync.dma_start(out=gt[r, h][:], in_=gate[r, h * P:(h + 1) * P, :])
+
+        words = [keep.tile([P, T], U32, name="words%d" % a, align_bytes=64) for a in range(PASSES)]
+        sbytes = keep.tile([P, T], U8, name="sbytes", align_bytes=64)
+        nc.gpsimd.memset(sbytes[:], 0)
+        gwords = [keep.tile([P, SLOTS], U32, name="gwords%d" % a, align_bytes=64) for a in range(PASSES)]
+        gbytes = keep.tile([P, SLOTS], U8, name="gbytes", align_bytes=64)
+
+        grouped = {}
+
+        def cast(a, lo, hi, vshare):
+            w = hi - lo
+            g = keep.tile([P, w, 4], BF16, name="grouped%d_%d" % (a, lo), align_bytes=64)
+            grouped[a, lo] = g
+            if vshare > 0:
+                nc.vector.tensor_copy(
+                    out=g[:, 0:vshare, :].rearrange("p (c i) t -> p c t i", i=4),
+                    in_=raw[a, lo][:, :, 0:vshare].rearrange("p t (c i) -> p c t i", i=4),
+                )
+            nc.scalar.copy(
+                out=g[:, vshare:w, :].rearrange("p (c i) t -> p c t i", i=4),
+                in_=raw[a, lo][:, :, vshare:w].rearrange("p t (c i) -> p c t i", i=4),
+            )
+
+        def quantise(a, lo, hi):
+            nc.vector.quantize_mx(
+                out=words[a][:, lo:hi].bitcast(FP8X4),
+                scales=sbytes[4 * a:P, lo:hi],
+                in_=grouped[a, lo][:].rearrange("p n t -> p (n t)"),
+            )
+
+        def gather(dst, window, lo, hi):
+            nc.vector.tensor_copy(out=dst[:, lo:hi], in_=window[:].indirect(offs_t[:, lo // 16:hi // 16]))
+
+        for a in range(PASSES):
+            for lo, hi, vshare in CHUNKS[a]:
+                cast(a, lo, hi, vshare)
+                quantise(a, lo, hi)
+        for lo, hi in zip(W0_CUTS[:-1], W0_CUTS[1:]):
+            gather(gwords[0], words[0], lo, hi)
+
+        y = [keep.tile([P, SLOTS], F32, name="y%d" % h) for h in range(HALVES)]
+        banks = {}
+        for h in range(HALVES):
+            for i in range(E // 2):
+                banks[h, i] = psum.tile([P, 2 * C], F32, name="bank%d%d" % (h, i))
+
+        def multiply(e, h, a):
+            nc.tensor.matmul_mx(
+                out=banks[h, e // 2][:, (e % 2) * C:(e % 2 + 1) * C],
+                lhsT=ww[e // 2][:, (e % 2) * PASSES + a, h * P:(h + 1) * P].bitcast(FP8X4),
+                lhsT_scale=ws[:, e * PASSES + a, h * P:(h + 1) * P],
+                rhs=gwords[a][:, e * C:(e + 1) * C].bitcast(FP8X4),
+                rhs_scale=gbytes[4 * a:P, e * C:(e + 1) * C],
+                start=(a == 0),
+                stop=(a == PASSES - 1),
+            )
+
+        for lo, hi in zip(W1_CUTS[:-1], W1_CUTS[1:]):
+            if lo in B_CUTS:
+                gather(gbytes, sbytes, lo, B_CUTS[lo])
+            gather(gwords[1], words[1], lo, hi)
+            for e in range(lo // C, hi // C):
+                for a in range(PASSES):
+                    for h in range(HALVES):
+                        multiply(e, h, a)
+                if e < E - 2:
+                    if e % 2 == 1:
+                        for h in range(HALVES):
+                            nc.scalar.copy(out=y[h][:, (e - 1) * C:(e + 1) * C], in_=banks[h, e // 2][:])
+                elif e == E - 2:
+                    for h in range(HALVES):
+                        nc.scalar.copy(out=y[h][:, e * C:(e + 1) * C], in_=banks[h, e // 2][:, 0:C])
+                else:
+                    nc.vector.tensor_copy(out=y[0][:, e * C:(e + 1) * C], in_=banks[0, e // 2][:, C:2 * C])
+                    nc.scalar.copy(out=y[1][:, e * C:(e + 1) * C], in_=banks[1, e // 2][:, C:2 * C])
+
+        ident = keep.tile([P, P], F32, name="ident")
+        make_identity(nc, ident[:])
+
+        def combine(h, lo, hi, accs):
+            w = hi - lo
+            t1 = keep.tile([P, w], F32, name="t1_%d_%d" % (h, lo))
+            t2 = keep.tile([P, w], F32, name="t2_%d_%d" % (h, lo))
+            o = keep.tile([P, w], F32, name="o_%d_%d" % (h, lo))
+            nc.vector.tensor_tensor(out=t1[:], in0=y[h][:].indirect(pos1_t[:, lo // 16:hi // 16]), in1=gt[0, h][:, lo:hi], op=MULT)
+            for acc in accs:
+                nc.tensor.matmul(out=acc[:, 0:w], lhsT=ident[:], rhs=t1[:], start=True, stop=False)
+            nc.vector.tensor_tensor(out=t2[:], in0=y[h][:].indirect(pos2_t[:, lo // 16:hi // 16]), in1=gt[1, h][:, lo:hi], op=MULT)
+            for acc in accs:
+                nc.tensor.matmul(out=acc[:, 0:w], lhsT=ident[:], rhs=t2[:], start=False, stop=True)
+                nc.scalar.copy(out=o[:], in_=acc[:, 0:w])
+                nc.scalar.dma_start(out=out[h * P:(h + 1) * P, lo:hi], in_=o[:])
+            if not accs:
+                for j in range(2):
+                    js = slice(j * w // 2, (j + 1) * w // 2)
+                    nc.vector.tensor_tensor(out=o[:, js], in0=t1[:, js], in1=t2[:, js], op=ADD)
+                    nc.sync.dma_start(out=out[h * P:(h + 1) * P, lo + j * w // 2:lo + (j + 1) * w // 2], in_=o[:, js])
+
+        combine(0, 0, T // 2, [banks[0, 0]])
+        combine(0, T // 2, T, [banks[0, 1]])
+        combine(1, 0, 384, [banks[0, 2]])
+        combine(1, 384, T, [])

@@ -114,9 +114,12 @@ def tile_routed_moe_kernel(tc, xT, w_words, w_scales, gate, offs, pos1, pos2, ou
             for i in range(E // 2):
                 banks[h, i] = psum.tile([P, 2 * C], F32, name="bank%d%d" % (h, i))
 
+        def group(e, h):
+            return banks[h, e % 4][:, (e // 4) * C:(e // 4 + 1) * C]
+
         def multiply(e, h, a):
             nc.tensor.matmul_mx(
-                out=banks[h, e // 2][:, (e % 2) * C:(e % 2 + 1) * C],
+                out=group(e, h),
                 lhsT=ww[e // 2][:, (e % 2) * PASSES + a, h * P:(h + 1) * P].bitcast(FP8X4),
                 lhsT_scale=ws[:, e * PASSES + a, h * P:(h + 1) * P],
                 rhs=gwords[a][:, e * C:(e + 1) * C].bitcast(FP8X4),
@@ -128,21 +131,17 @@ def tile_routed_moe_kernel(tc, xT, w_words, w_scales, gate, offs, pos1, pos2, ou
         for lo, hi in zip(W1_CUTS[:-1], W1_CUTS[1:]):
             if lo in B_CUTS:
                 gather(gbytes, sbytes, lo, B_CUTS[lo])
+                for e in range(lo // C, B_CUTS[lo] // C):
+                    for h in range(HALVES):
+                        multiply(e, h, 0)
             gather(gwords[1], words[1], lo, hi)
             for e in range(lo // C, hi // C):
-                for a in range(PASSES):
-                    for h in range(HALVES):
-                        multiply(e, h, a)
-                if e < E - 2:
-                    if e % 2 == 1:
-                        for h in range(HALVES):
-                            nc.scalar.copy(out=y[h][:, (e - 1) * C:(e + 1) * C], in_=banks[h, e // 2][:])
-                elif e == E - 2:
-                    for h in range(HALVES):
-                        nc.scalar.copy(out=y[h][:, e * C:(e + 1) * C], in_=banks[h, e // 2][:, 0:C])
-                else:
-                    nc.vector.tensor_copy(out=y[0][:, e * C:(e + 1) * C], in_=banks[0, e // 2][:, C:2 * C])
-                    nc.scalar.copy(out=y[1][:, e * C:(e + 1) * C], in_=banks[1, e // 2][:, C:2 * C])
+                for h in range(HALVES):
+                    multiply(e, h, 1)
+                    if e == E - 1 and h == 0:
+                        nc.vector.tensor_copy(out=y[h][:, e * C:(e + 1) * C], in_=group(e, h))
+                    else:
+                        nc.scalar.copy(out=y[h][:, e * C:(e + 1) * C], in_=group(e, h))
 
         ident = keep.tile([P, P], F32, name="ident")
         make_identity(nc, ident[:])

@@ -22,7 +22,7 @@ SLOTS = E * C
 CH = 512
 NCH = T // CH
 HALVES = N // P
-CHUNKS = (((0, 512, 336), (512, 768, 168), (768, 1024, 200)), ((0, 512, 0), (512, 1024, 176)))
+CHUNKS = (((0, 512, 336), (512, 768, 168), (768, 1024, 200)), ((0, 256, 0), (256, 512, 0), (512, 768, 0), (768, 1024, 0)))
 W0_CUTS = (0, 768, 1536, 2048)
 W1_CUTS = (0, 768, 1536, 1792, 2048)
 B_CUTS = {0: 768, 768: 1536, 1536: 2048}

@@ -138,10 +138,7 @@ def tile_routed_moe_kernel(tc, xT, w_words, w_scales, gate, offs, pos1, pos2, ou
             for e in range(lo // C, hi // C):
                 for h in range(HALVES):
                     multiply(e, h, 1)
-                    if e == E - 1 and h == 0:
-                        nc.vector.tensor_copy(out=y[h][:, e * C:(e + 1) * C], in_=group(e, h))
-                    else:
-                        nc.scalar.copy(out=y[h][:, e * C:(e + 1) * C], in_=group(e, h))
+                    nc.scalar.copy(out=y[h][:, e * C:(e + 1) * C], in_=group(e, h))
 
         ident = keep.tile([P, P], F32, name="ident")
         make_identity(nc, ident[:])
@@ -154,7 +151,9 @@ def tile_routed_moe_kernel(tc, xT, w_words, w_scales, gate, offs, pos1, pos2, ou
             nc.vector.tensor_tensor(out=t1[:], in0=y[h][:].indirect(pos1_t[:, lo // 16:hi // 16]), in1=gt[0, h][:, lo:hi], op=MULT)
             for acc in accs:
                 nc.tensor.matmul(out=acc[:, 0:w], lhsT=ident[:], rhs=t1[:], start=True, stop=False)
-            nc.vector.tensor_tensor(out=t2[:], in0=y[h][:].indirect(pos2_t[:, lo // 16:hi // 16]), in1=gt[1, h][:, lo:hi], op=MULT)
+            cuts = (lo, hi) if accs else (lo, (lo + hi) // 2, hi)
+            for c0, c1 in zip(cuts[:-1], cuts[1:]):
+                nc.vector.tensor_tensor(out=t2[:, c0 - lo:c1 - lo], in0=y[h][:].indirect(pos2_t[:, c0 // 16:c1 // 16]), in1=gt[1, h][:, c0:c1], op=MULT)
             for acc in accs:
                 nc.tensor.matmul(out=acc[:, 0:w], lhsT=ident[:], rhs=t2[:], start=False, stop=True)
                 nc.scalar.copy(out=o[:], in_=acc[:, 0:w])

@@ -136,9 +136,12 @@ def tile_routed_moe_kernel(tc, xT, w_words, w_scales, gate, offs, pos1, pos2, ou
                         multiply(e, h, 0)
             gather(gwords[1], words[1], lo, hi)
             for e in range(lo // C, hi // C):
-                for h in range(HALVES):
-                    multiply(e, h, 1)
-                    nc.scalar.copy(out=y[h][:, e * C:(e + 1) * C], in_=group(e, h))
+                multiply(e, 0, 1)
+                nc.scalar.copy(out=y[0][:, e * C:(e + 1) * C], in_=group(e, 0))
+            for e in range(lo // C, hi // C):
+                multiply(e, 1, 1)
+        for e in range(E):
+            nc.scalar.copy(out=y[1][:, e * C:(e + 1) * C], in_=group(e, 1))
 
         ident = keep.tile([P, P], F32, name="ident")
         make_identity(nc, ident[:])

@@ -26,6 +26,7 @@ CHUNKS = (((0, 512, 336), (512, 768, 168), (768, 1024, 200)), ((0, 256, 0), (256
 W0_CUTS = (0, 768, 1536, 2048)
 W1_CUTS = (0, 768, 1536, 1792, 2048)
 B_CUTS = {0: 768, 768: 1536, 1536: 2048}
+PIECES = ((0, 0, 512), (0, 512, 1024), (1, 0, 384), (1, 384, 1024))
 
 
 def tile_routed_moe_kernel(tc, xT, w_words, w_scales, gate, offs, pos1, pos2, out):
@@ -64,10 +65,10 @@ def tile_routed_moe_kernel(tc, xT, w_words, w_scales, gate, offs, pos1, pos2, ou
         nc.sync.dma_start(pos1_t[:], pos1)
         nc.sync.dma_start(pos2_t[:], pos2)
         gt = {}
-        for h in range(HALVES):
+        for h, lo, hi in PIECES:
             for r in range(2):
-                gt[r, h] = keep.tile([P, T], F32, name="gate%d%d" % (r, h))
-                nc.sync.dma_start(out=gt[r, h][:], in_=gate[r, h * P:(h + 1) * P, :])
+                gt[r, h, lo] = keep.tile([P, hi - lo], F32, name="gate%d%d_%d" % (r, h, lo))
+                nc.sync.dma_start(out=gt[r, h, lo][:], in_=gate[r, h * P:(h + 1) * P, lo:hi])
 
         words = [keep.tile([P, T], U32, name="words%d" % a, align_bytes=64) for a in range(PASSES)]
         sbytes = keep.tile([P, T], U8, name="sbytes", align_bytes=64)
@@ -151,12 +152,12 @@ def tile_routed_moe_kernel(tc, xT, w_words, w_scales, gate, offs, pos1, pos2, ou
             t1 = keep.tile([P, w], F32, name="t1_%d_%d" % (h, lo))
             t2 = keep.tile([P, w], F32, name="t2_%d_%d" % (h, lo))
             o = keep.tile([P, w], F32, name="o_%d_%d" % (h, lo))
-            nc.vector.tensor_tensor(out=t1[:], in0=y[h][:].indirect(pos1_t[:, lo // 16:hi // 16]), in1=gt[0, h][:, lo:hi], op=MULT)
+            nc.vector.tensor_tensor(out=t1[:], in0=y[h][:].indirect(pos1_t[:, lo // 16:hi // 16]), in1=gt[0, h, lo][:], op=MULT)
             for acc in accs:
                 nc.tensor.matmul(out=acc[:, 0:w], lhsT=ident[:], rhs=t1[:], start=True, stop=False)
             cuts = (lo, hi) if accs else (lo, (lo + hi) // 2, hi)
             for c0, c1 in zip(cuts[:-1], cuts[1:]):
-                nc.vector.tensor_tensor(out=t2[:, c0 - lo:c1 - lo], in0=y[h][:].indirect(pos2_t[:, c0 // 16:c1 // 16]), in1=gt[1, h][:, c0:c1], op=MULT)
+                nc.vector.tensor_tensor(out=t2[:, c0 - lo:c1 - lo], in0=y[h][:].indirect(pos2_t[:, c0 // 16:c1 // 16]), in1=gt[1, h, lo][:, c0 - lo:c1 - lo], op=MULT)
             for acc in accs:
                 nc.tensor.matmul(out=acc[:, 0:w], lhsT=ident[:], rhs=t2[:], start=False, stop=True)
                 nc.scalar.copy(out=o[:], in_=acc[:, 0:w])

@@ -22,7 +22,7 @@ SLOTS = E * C
 CH = 512
 NCH = T // CH
 HALVES = N // P
-CHUNKS = (((0, 512, 336), (512, 768, 168), (768, 1024, 200)), ((0, 256, 0), (256, 512, 0), (512, 768, 0), (768, 1024, 0)))
+CHUNKS = (((0, 512, 336), (512, 768, 168), (768, 1024, 200)), ((0, 256, 0), (256, 512, 0), (512, 768, 0), (768, 1024, 64)))
 W0_CUTS = (0, 768, 1536, 2048)
 W1_CUTS = (0, 768, 1536, 1792, 2048)
 B_CUTS = {0: 768, 768: 1536, 1536: 2048}
@@ -102,10 +102,13 @@ def tile_routed_moe_kernel(tc, xT, w_words, w_scales, gate, offs, pos1, pos2, ou
         def gather(dst, window, lo, hi):
             nc.vector.tensor_copy(out=dst[:, lo:hi], in_=window[:].indirect(offs_t[:, lo // 16:hi // 16]))
 
-        for a in range(PASSES):
-            for lo, hi, vshare in CHUNKS[a]:
-                cast(a, lo, hi, vshare)
-                quantise(a, lo, hi)
+        for lo, hi, vshare in CHUNKS[0]:
+            cast(0, lo, hi, vshare)
+            quantise(0, lo, hi)
+        for lo, hi, vshare in CHUNKS[1]:
+            cast(1, lo, hi, vshare)
+        for lo, hi, vshare in CHUNKS[1]:
+            quantise(1, lo, hi)
         for lo, hi in zip(W0_CUTS[:-1], W0_CUTS[1:]):
             gather(gwords[0], words[0], lo, hi)
 

@@ -107,10 +107,10 @@ def tile_routed_moe_kernel(tc, xT, w_words, w_scales, gate, offs, pos1, pos2, ou
             quantise(0, lo, hi)
         for lo, hi, vshare in CHUNKS[1]:
             cast(1, lo, hi, vshare)
-        for lo, hi, vshare in CHUNKS[1]:
-            quantise(1, lo, hi)
         for lo, hi in zip(W0_CUTS[:-1], W0_CUTS[1:]):
             gather(gwords[0], words[0], lo, hi)
+        for lo, hi, vshare in CHUNKS[1]:
+            quantise(1, lo, hi)
 
         y = [keep.tile([P, SLOTS], F32, name="y%d" % h) for h in range(HALVES)]
         banks = {}

@@ -22,7 +22,7 @@ SLOTS = E * C
 CH = 512
 NCH = T // CH
 HALVES = N // P
-CHUNKS = (((0, 512, 336), (512, 768, 168), (768, 1024, 200)), ((0, 256, 0), (256, 512, 0), (512, 768, 0), (768, 1024, 64)))
+CHUNKS = (((0, 256, 152), (256, 512, 152), (512, 768, 152), (768, 1024, 168)), ((0, 256, 0), (256, 512, 0), (512, 768, 0), (768, 1024, 64)))
 W0_CUTS = (0, 768, 1536, 2048)
 W1_CUTS = (0, 768, 1536, 1792, 2048)
 B_CUTS = {0: 768, 768: 1536, 1536: 2048}
@@ -40,14 +40,22 @@ def tile_routed_moe_kernel(tc, xT, w_words, w_scales, gate, offs, pos1, pos2, ou
         pos1_t = lists.tile([P, T // 16], U16, name="pos1_t")
         pos2_t = lists.tile([P, T // 16], U16, name="pos2_t")
 
+        primer = keep.tile([P, 2], F32, name="primer")
+        nc.gpsimd.memset(primer[:], 0.0)
+        nc.scalar.copy(out=primer[:, 1:2], in_=primer[:, 0:1])
+
         xv = xT.rearrange("(a p t) n -> a p t n", p=P, t=4)
         raw = {}
-        for a in range(PASSES):
-            for lo, hi, vshare in CHUNKS[a]:
-                raw[a, lo] = keep.tile([P, 4, hi - lo], F32, name="raw%d_%d" % (a, lo))
-                nc.sync.dma_start(out=raw[a, lo][:], in_=xv[a, :, :, lo:hi])
-                if a == 0 and lo == 0:
-                    nc.sync.dma_start(offs_t[:], offs)
+        raw0 = keep.tile([P, 4, T], F32, name="raw0")
+        nc.sync.dma_start(out=raw0[:, 0:2, :], in_=xv[0, :, 0:2, :])
+        nc.sync.dma_start(offs_t[:], offs)
+        for lo, hi, vshare in CHUNKS[0]:
+            raw[0, lo] = raw0[:, :, lo:hi]
+            nc.sync.dma_start(out=raw0[:, 2:4, lo:hi], in_=xv[0, :, 2:4, lo:hi])
+        for lo, hi, vshare in CHUNKS[1]:
+            raw1 = keep.tile([P, 4, hi - lo], F32, name="raw1_%d" % lo)
+            raw[1, lo] = raw1[:]
+            nc.sync.dma_start(out=raw1[:], in_=xv[1, :, :, lo:hi])
 
         ws = keep.tile([P, E * PASSES, N], U8, name="ws", align_bytes=64)
         nc.vector.memset(ws[:].rearrange("p g n -> p (g n)").bitcast(I32), 0)

@@ -86,19 +86,21 @@ def tile_routed_moe_kernel(tc, xT, w_words, w_scales, gate, offs, pos1, pos2, ou
 
         grouped = {}
 
-        def cast(a, lo, hi, vshare):
-            w = hi - lo
-            g = keep.tile([P, w, 4], BF16, name="grouped%d_%d" % (a, lo), align_bytes=64)
-            grouped[a, lo] = g
-            if vshare > 0:
-                nc.vector.tensor_copy(
-                    out=g[:, 0:vshare, :].rearrange("p (c i) t -> p c t i", i=4),
-                    in_=raw[a, lo][:, :, 0:vshare].rearrange("p t (c i) -> p c t i", i=4),
-                )
-            nc.scalar.copy(
-                out=g[:, vshare:w, :].rearrange("p (c i) t -> p c t i", i=4),
-                in_=raw[a, lo][:, :, vshare:w].rearrange("p t (c i) -> p c t i", i=4),
+        for a in range(PASSES):
+            for lo, hi, vshare in CHUNKS[a]:
+                grouped[a, lo] = keep.tile([P, hi - lo, 4], BF16, name="grouped%d_%d" % (a, lo), align_bytes=64)
+
+        def interleave(copy, a, lo, c0, c1):
+            copy(
+                out=grouped[a, lo][:, c0:c1, :].rearrange("p (c i) t -> p c t i", i=4),
+                in_=raw[a, lo][:, :, c0:c1].rearrange("p t (c i) -> p c t i", i=4),
             )
+
+        def cast_vector(a, lo, hi, vshare):
+            interleave(nc.vector.tensor_copy, a, lo, 0, vshare)
+
+        def cast_scalar(a, lo, hi, vshare):
+            interleave(nc.scalar.copy, a, lo, vshare, hi - lo)
 
         def quantise(a, lo, hi):
             nc.vector.quantize_mx(
@@ -111,14 +113,18 @@ def tile_routed_moe_kernel(tc, xT, w_words, w_scales, gate, offs, pos1, pos2, ou
             nc.vector.tensor_copy(out=dst[:, lo:hi], in_=window[:].indirect(offs_t[:, lo // 16:hi // 16]))
 
         for lo, hi, vshare in CHUNKS[0]:
-            cast(0, lo, hi, vshare)
+            cast_vector(0, lo, hi, vshare)
+            cast_scalar(0, lo, hi, vshare)
             quantise(0, lo, hi)
         for lo, hi, vshare in CHUNKS[1]:
-            cast(1, lo, hi, vshare)
+            cast_scalar(1, lo, hi, vshare)
         for lo, hi in zip(W0_CUTS[:-1], W0_CUTS[1:]):
             gather(gwords[0], words[0], lo, hi)
-        for lo, hi, vshare in CHUNKS[1]:
-            quantise(1, lo, hi)
+        quantise(1, *CHUNKS[1][0][:2])
+        quantise(1, *CHUNKS[1][1][:2])
+        cast_vector(1, *CHUNKS[1][3])
+        quantise(1, *CHUNKS[1][2][:2])
+        quantise(1, *CHUNKS[1][3][:2])
 
         y = [keep.tile([P, SLOTS], F32, name="y%d" % h) for h in range(HALVES)]
         banks = {}

@@ -46,14 +46,14 @@ def tile_routed_moe_kernel(tc, xT, w_words, w_scales, gate, offs, pos1, pos2, ou
 
         xv = xT.rearrange("(a p t) n -> a p t n", p=P, t=4)
         raw = {}
-        raw0 = keep.tile([P, 4, T], F32, name="raw0")
+        raw0 = keep.tile([P, 4, T], F32, name="raw0", align_bytes=256)
         nc.sync.dma_start(out=raw0[:, 0:2, :], in_=xv[0, :, 0:2, :])
         nc.sync.dma_start(offs_t[:], offs)
         for lo, hi, vshare in CHUNKS[0]:
             raw[0, lo] = raw0[:, :, lo:hi]
             nc.sync.dma_start(out=raw0[:, 2:4, lo:hi], in_=xv[0, :, 2:4, lo:hi])
         for lo, hi, vshare in CHUNKS[1]:
-            raw1 = keep.tile([P, 4, hi - lo], F32, name="raw1_%d" % lo)
+            raw1 = keep.tile([P, 4, hi - lo], F32, name="raw1_%d" % lo, align_bytes=256)
             raw[1, lo] = raw1[:]
             nc.sync.dma_start(out=raw1[:], in_=xv[1, :, :, lo:hi])
 
@@ -67,7 +67,7 @@ def tile_routed_moe_kernel(tc, xT, w_words, w_scales, gate, offs, pos1, pos2, ou
         wv = w_words.rearrange("e a p n r -> p (e a) (n r)").bitcast(I32)
         ww = []
         for i in range(E // 2):
-            wt = keep.tile([P, 2 * PASSES, N], I32, name="ww%d" % i, align_bytes=64)
+            wt = keep.tile([P, 2 * PASSES, N], I32, name="ww%d" % i, align_bytes=256)
             nc.sync.dma_start(out=wt[:], in_=wv[:, 2 * PASSES * i:2 * PASSES * (i + 1), :])
             ww.append(wt)
         nc.sync.dma_start(pos1_t[:], pos1)
@@ -75,7 +75,7 @@ def tile_routed_moe_kernel(tc, xT, w_words, w_scales, gate, offs, pos1, pos2, ou
         gt = {}
         for h, lo, hi in PIECES:
             for r in range(2):
-                gt[r, h, lo] = keep.tile([P, hi - lo], F32, name="gate%d%d_%d" % (r, h, lo))
+                gt[r, h, lo] = keep.tile([P, hi - lo], F32, name="gate%d%d_%d" % (r, h, lo), align_bytes=256)
                 nc.sync.dma_start(out=gt[r, h, lo][:], in_=gate[r, h * P:(h + 1) * P, lo:hi])
 
         words = [keep.tile([P, T], U32, name="words%d" % a, align_bytes=64) for a in range(PASSES)]

@@ -22,10 +22,11 @@ SLOTS = E * C
 CH = 512
 NCH = T // CH
 HALVES = N // P
-CHUNKS = (((0, 256, 152), (256, 512, 152), (512, 768, 152), (768, 1024, 168)), ((0, 256, 0), (256, 512, 0), (512, 768, 0), (768, 1024, 64)))
+CHUNKS = (((0, 256, 152), (256, 512, 152), (512, 768, 152), (768, 1024, 168)), ((0, 256, 0), (256, 512, 0), (512, 768, 0), (768, 1024, 0)))
 W0_CUTS = (0, 768, 1536, 2048)
 W1_CUTS = (0, 768, 1536, 1792, 2048)
 B_CUTS = {0: 768, 768: 1536, 1536: 2048}
+LATE = ((6, 1), (7, 1))
 PIECES = ((0, 0, 512), (0, 512, 1024), (1, 0, 384), (1, 384, 1024))
 
 
@@ -48,10 +49,10 @@ def tile_routed_moe_kernel(tc, xT, w_words, w_scales, gate, offs, pos1, pos2, ou
         raw = {}
         raw0 = keep.tile([P, 4, T], F32, name="raw0", align_bytes=256)
         nc.sync.dma_start(out=raw0[:, 0:2, :], in_=xv[0, :, 0:2, :])
-        nc.sync.dma_start(offs_t[:], offs)
         for lo, hi, vshare in CHUNKS[0]:
             raw[0, lo] = raw0[:, :, lo:hi]
             nc.sync.dma_start(out=raw0[:, 2:4, lo:hi], in_=xv[0, :, 2:4, lo:hi])
+        nc.sync.dma_start(offs_t[:], offs)
         for lo, hi, vshare in CHUNKS[1]:
             raw1 = keep.tile([P, 4, hi - lo], F32, name="raw1_%d" % lo, align_bytes=256)
             raw[1, lo] = raw1[:]
@@ -122,7 +123,6 @@ def tile_routed_moe_kernel(tc, xT, w_words, w_scales, gate, offs, pos1, pos2, ou
             gather(gwords[0], words[0], lo, hi)
         quantise(1, *CHUNKS[1][0][:2])
         quantise(1, *CHUNKS[1][1][:2])
-        cast_vector(1, *CHUNKS[1][3])
         quantise(1, *CHUNKS[1][2][:2])
         quantise(1, *CHUNKS[1][3][:2])
 
@@ -133,6 +133,8 @@ def tile_routed_moe_kernel(tc, xT, w_words, w_scales, gate, offs, pos1, pos2, ou
                 banks[h, i] = psum.tile([P, 2 * C], F32, name="bank%d%d" % (h, i))
 
         def group(e, h):
+            if (e, h) in LATE:
+                return banks[0, 3][:, (e - 6) * C:(e - 5) * C]
             return banks[h, e % 4][:, (e // 4) * C:(e // 4 + 1) * C]
 
         def multiply(e, h, a):
@@ -151,13 +153,18 @@ def tile_routed_moe_kernel(tc, xT, w_words, w_scales, gate, offs, pos1, pos2, ou
                 gather(gbytes, sbytes, lo, B_CUTS[lo])
                 for e in range(lo // C, B_CUTS[lo] // C):
                     for h in range(HALVES):
-                        multiply(e, h, 0)
+                        if (e, h) not in LATE:
+                            multiply(e, h, 0)
             gather(gwords[1], words[1], lo, hi)
             for e in range(lo // C, hi // C):
                 multiply(e, 0, 1)
                 nc.scalar.copy(out=y[0][:, e * C:(e + 1) * C], in_=group(e, 0))
             for e in range(lo // C, hi // C):
-                multiply(e, 1, 1)
+                if (e, 1) not in LATE:
+                    multiply(e, 1, 1)
+        for e, h in LATE:
+            multiply(e, h, 0)
+            multiply(e, h, 1)
         for e in range(E):
             nc.scalar.copy(out=y[1][:, e * C:(e + 1) * C], in_=group(e, 1))
 

@@ -22,7 +22,7 @@ SLOTS = E * C
 CH = 512
 NCH = T // CH
 HALVES = N // P
-CHUNKS = (((0, 256, 152), (256, 512, 152), (512, 768, 152), (768, 1024, 168)), ((0, 256, 0), (256, 512, 0), (512, 768, 0), (768, 1024, 0)))
+CHUNKS = (((0, 256, 152), (256, 512, 152), (512, 768, 152), (768, 1024, 168)), ((0, 256, 0), (256, 512, 0), (512, 768, 0), (768, 1024, 64)))
 W0_CUTS = (0, 768, 1536, 2048)
 W1_CUTS = (0, 768, 1536, 1792, 2048)
 B_CUTS = {0: 768, 768: 1536, 1536: 2048}
@@ -91,17 +91,17 @@ def tile_routed_moe_kernel(tc, xT, w_words, w_scales, gate, offs, pos1, pos2, ou
             for lo, hi, vshare in CHUNKS[a]:
                 grouped[a, lo] = keep.tile([P, hi - lo, 4], BF16, name="grouped%d_%d" % (a, lo), align_bytes=64)
 
-        def interleave(copy, a, lo, c0, c1):
+        def interleave(copy, a, lo, c0, c1, rows):
             copy(
-                out=grouped[a, lo][:, c0:c1, :].rearrange("p (c i) t -> p c t i", i=4),
-                in_=raw[a, lo][:, :, c0:c1].rearrange("p t (c i) -> p c t i", i=4),
+                out=grouped[a, lo][:, c0:c1, rows].rearrange("p (c i) t -> p c t i", i=4),
+                in_=raw[a, lo][:, rows, c0:c1].rearrange("p t (c i) -> p c t i", i=4),
             )
 
-        def cast_vector(a, lo, hi, vshare):
-            interleave(nc.vector.tensor_copy, a, lo, 0, vshare)
+        def cast_vector(a, lo, hi, vshare, rows=slice(0, 4)):
+            interleave(nc.vector.tensor_copy, a, lo, 0, vshare, rows)
 
-        def cast_scalar(a, lo, hi, vshare):
-            interleave(nc.scalar.copy, a, lo, vshare, hi - lo)
+        def cast_scalar(a, lo, hi, vshare, rows=slice(0, 4)):
+            interleave(nc.scalar.copy, a, lo, vshare, hi - lo, rows)
 
         def quantise(a, lo, hi):
             nc.vector.quantize_mx(
@@ -113,9 +113,13 @@ def tile_routed_moe_kernel(tc, xT, w_words, w_scales, gate, offs, pos1, pos2, ou
         def gather(dst, window, lo, hi):
             nc.vector.tensor_copy(out=dst[:, lo:hi], in_=window[:].indirect(offs_t[:, lo // 16:hi // 16]))
 
+        last = CHUNKS[0][-1]
+        cast_vector(0, *last, slice(0, 2))
+        cast_scalar(0, *last, slice(0, 2))
         for lo, hi, vshare in CHUNKS[0]:
-            cast_vector(0, lo, hi, vshare)
-            cast_scalar(0, lo, hi, vshare)
+            rows = slice(2, 4) if lo == last[0] else slice(0, 4)
+            cast_vector(0, lo, hi, vshare, rows)
+            cast_scalar(0, lo, hi, vshare, rows)
             quantise(0, lo, hi)
         for lo, hi, vshare in CHUNKS[1]:
             cast_scalar(1, lo, hi, vshare)
@@ -123,6 +127,7 @@ def tile_routed_moe_kernel(tc, xT, w_words, w_scales, gate, offs, pos1, pos2, ou
             gather(gwords[0], words[0], lo, hi)
         quantise(1, *CHUNKS[1][0][:2])
         quantise(1, *CHUNKS[1][1][:2])
+        cast_vector(1, *CHUNKS[1][3])
         quantise(1, *CHUNKS[1][2][:2])
         quantise(1, *CHUNKS[1][3][:2])
 

from contextlib import ExitStack

import concourse.mybir as mybir
from concourse.masks import make_identity

K, T, E, C, N = 1024, 1024, 8, 256, 256
FLOPS = 2 * K * N * E * C

F32 = mybir.dt.float32
BF16 = mybir.dt.bfloat16
I32 = mybir.dt.int32
U32 = mybir.dt.uint32
U16 = mybir.dt.uint16
U8 = mybir.dt.uint8
FP8X4 = mybir.dt.float8_e4m3fn_x4
MULT = mybir.AluOpType.mult
ADD = mybir.AluOpType.add

P = 128
PASSES = K // 512
SLOTS = E * C
CH = 512
NCH = T // CH
HALVES = N // P
CHUNKS = (((0, 256, 152), (256, 512, 152), (512, 768, 152), (768, 1024, 168)), ((0, 256, 0), (256, 512, 0), (512, 768, 0), (768, 1024, 64)))
W0_CUTS = (0, 768, 1536, 2048)
W1_CUTS = (0, 768, 1536, 1792, 2048)
B_CUTS = {0: 768, 768: 1536, 1536: 2048}
LATE = ((6, 1), (7, 1))
PIECES = ((0, 0, 512), (0, 512, 1024), (1, 0, 384), (1, 384, 1024))


def tile_routed_moe_kernel(tc, xT, w_words, w_scales, gate, offs, pos1, pos2, out):
    nc = tc.nc
    with ExitStack() as ctx:
        lists = ctx.enter_context(tc.tile_pool(name="lists", bufs=1))
        keep = ctx.enter_context(tc.tile_pool(name="keep", bufs=1))
        psum = ctx.enter_context(tc.psum_pool(name="psum", bufs=1))

        offs_t = lists.tile([P, SLOTS // 16], U16, name="offs_t")
        pos1_t = lists.tile([P, T // 16], U16, name="pos1_t")
        pos2_t = lists.tile([P, T // 16], U16, name="pos2_t")

        primer = keep.tile([P, 2], F32, name="primer")
        nc.gpsimd.memset(primer[:], 0.0)
        nc.scalar.copy(out=primer[:, 1:2], in_=primer[:, 0:1])

        xv = xT.rearrange("(a p t) n -> a p t n", p=P, t=4)
        raw = {}
        raw0 = keep.tile([P, 4, T], F32, name="raw0", align_bytes=256)
        nc.sync.dma_start(out=raw0[:, 0:2, :], in_=xv[0, :, 0:2, :])
        for lo, hi, vshare in CHUNKS[0]:
            raw[0, lo] = raw0[:, :, lo:hi]
            nc.sync.dma_start(out=raw0[:, 2:4, lo:hi], in_=xv[0, :, 2:4, lo:hi])
        nc.sync.dma_start(offs_t[:], offs)
        for lo, hi, vshare in CHUNKS[1]:
            raw1 = keep.tile([P, 4, hi - lo], F32, name="raw1_%d" % lo, align_bytes=256)
            raw[1, lo] = raw1[:]
            nc.sync.dma_start(out=raw1[:], in_=xv[1, :, :, lo:hi])

        ws = keep.tile([P, E * PASSES, N], U8, name="ws", align_bytes=64)
        nc.vector.memset(ws[:].rearrange("p g n -> p (g n)").bitcast(I32), 0)
        for q in range(4):
            nc.sync.dma_start(
                out=ws[32 * q:32 * q + 4, :, :].bitcast(I32),
                in_=w_scales[:, :, 4 * q:4 * q + 4, :].rearrange("e a r n -> r (e a) n").bitcast(I32),
            )
        wv = w_words.rearrange("e a p n r -> p (e a) (n r)").bitcast(I32)
        ww = []
        for i in range(E // 2):
            wt = keep.tile([P, 2 * PASSES, N], I32, name="ww%d" % i, align_bytes=256)
            nc.sync.dma_start(out=wt[:], in_=wv[:, 2 * PASSES * i:2 * PASSES * (i + 1), :])
            ww.append(wt)
        nc.sync.dma_start(pos1_t[:], pos1)
        nc.sync.dma_start(pos2_t[:], pos2)
        gt = {}
        for h, lo, hi in PIECES:
            for r in range(2):
                gt[r, h, lo] = keep.tile([P, hi - lo], F32, name="gate%d%d_%d" % (r, h, lo), align_bytes=256)
                nc.sync.dma_start(out=gt[r, h, lo][:], in_=gate[r, h * P:(h + 1) * P, lo:hi])

        words = [keep.tile([P, T], U32, name="words%d" % a, align_bytes=64) for a in range(PASSES)]
        sbytes = keep.tile([P, T], U8, name="sbytes", align_bytes=64)
        nc.gpsimd.memset(sbytes[:], 0)
        gwords = [keep.tile([P, SLOTS], U32, name="gwords%d" % a, align_bytes=64) for a in range(PASSES)]
        gbytes = keep.tile([P, SLOTS], U8, name="gbytes", align_bytes=64)

        grouped = {}

        for a in range(PASSES):
            for lo, hi, vshare in CHUNKS[a]:
                grouped[a, lo] = keep.tile([P, hi - lo, 4], BF16, name="grouped%d_%d" % (a, lo), align_bytes=64)

        def interleave(copy, a, lo, c0, c1, rows):
            copy(
                out=grouped[a, lo][:, c0:c1, rows].rearrange("p (c i) t -> p c t i", i=4),
                in_=raw[a, lo][:, rows, c0:c1].rearrange("p t (c i) -> p c t i", i=4),
            )

        def cast_vector(a, lo, hi, vshare, rows=slice(0, 4)):
            interleave(nc.vector.tensor_copy, a, lo, 0, vshare, rows)

        def cast_scalar(a, lo, hi, vshare, rows=slice(0, 4)):
            interleave(nc.scalar.copy, a, lo, vshare, hi - lo, rows)

        def quantise(a, lo, hi):
            nc.vector.quantize_mx(
                out=words[a][:, lo:hi].bitcast(FP8X4),
                scales=sbytes[4 * a:P, lo:hi],
                in_=grouped[a, lo][:].rearrange("p n t -> p (n t)"),
            )

        def gather(dst, window, lo, hi):
            nc.vector.tensor_copy(out=dst[:, lo:hi], in_=window[:].indirect(offs_t[:, lo // 16:hi // 16]))

        last = CHUNKS[0][-1]
        cast_vector(0, *last, slice(0, 2))
        cast_scalar(0, *last, slice(0, 2))
        for lo, hi, vshare in CHUNKS[0]:
            rows = slice(2, 4) if lo == last[0] else slice(0, 4)
            cast_vector(0, lo, hi, vshare, rows)
            cast_scalar(0, lo, hi, vshare, rows)
            quantise(0, lo, hi)
        for lo, hi, vshare in CHUNKS[1]:
            cast_scalar(1, lo, hi, vshare)
        for lo, hi in zip(W0_CUTS[:-1], W0_CUTS[1:]):
            gather(gwords[0], words[0], lo, hi)
        quantise(1, *CHUNKS[1][0][:2])
        quantise(1, *CHUNKS[1][1][:2])
        cast_vector(1, *CHUNKS[1][3])
        quantise(1, *CHUNKS[1][2][:2])
        quantise(1, *CHUNKS[1][3][:2])

        y = [keep.tile([P, SLOTS], F32, name="y%d" % h) for h in range(HALVES)]
        banks = {}
        for h in range(HALVES):
            for i in range(E // 2):
                banks[h, i] = psum.tile([P, 2 * C], F32, name="bank%d%d" % (h, i))

        def group(e, h):
            if (e, h) in LATE:
                return banks[0, 3][:, (e - 6) * C:(e - 5) * C]
            return banks[h, e % 4][:, (e // 4) * C:(e // 4 + 1) * C]

        def multiply(e, h, a):
            nc.tensor.matmul_mx(
                out=group(e, h),
                lhsT=ww[e // 2][:, (e % 2) * PASSES + a, h * P:(h + 1) * P].bitcast(FP8X4),
                lhsT_scale=ws[:, e * PASSES + a, h * P:(h + 1) * P],
                rhs=gwords[a][:, e * C:(e + 1) * C].bitcast(FP8X4),
                rhs_scale=gbytes[4 * a:P, e * C:(e + 1) * C],
                start=(a == 0),
                stop=(a == PASSES - 1),
            )

        for lo, hi in zip(W1_CUTS[:-1], W1_CUTS[1:]):
            if lo in B_CUTS:
                gather(gbytes, sbytes, lo, B_CUTS[lo])
                for e in range(lo // C, B_CUTS[lo] // C):
                    for h in range(HALVES):
                        if (e, h) not in LATE:
                            multiply(e, h, 0)
            gather(gwords[1], words[1], lo, hi)
            for e in range(lo // C, hi // C):
                multiply(e, 0, 1)
                nc.scalar.copy(out=y[0][:, e * C:(e + 1) * C], in_=group(e, 0))
            for e in range(lo // C, hi // C):
                if (e, 1) not in LATE:
                    multiply(e, 1, 1)
        for e, h in LATE:
            multiply(e, h, 0)
            multiply(e, h, 1)
        for e in range(E):
            nc.scalar.copy(out=y[1][:, e * C:(e + 1) * C], in_=group(e, 1))

        ident = keep.tile([P, P], F32, name="ident")
        make_identity(nc, ident[:])

        def combine(h, lo, hi, accs):
            w = hi - lo
            t1 = keep.tile([P, w], F32, name="t1_%d_%d" % (h, lo))
            t2 = keep.tile([P, w], F32, name="t2_%d_%d" % (h, lo))
            o = keep.tile([P, w], F32, name="o_%d_%d" % (h, lo))
            nc.vector.tensor_tensor(out=t1[:], in0=y[h][:].indirect(pos1_t[:, lo // 16:hi // 16]), in1=gt[0, h, lo][:], op=MULT)
            for acc in accs:
                nc.tensor.matmul(out=acc[:, 0:w], lhsT=ident[:], rhs=t1[:], start=True, stop=False)
            cuts = (lo, hi) if accs else (lo, (lo + hi) // 2, hi)
            for c0, c1 in zip(cuts[:-1], cuts[1:]):
                nc.vector.tensor_tensor(out=t2[:, c0 - lo:c1 - lo], in0=y[h][:].indirect(pos2_t[:, c0 // 16:c1 // 16]), in1=gt[1, h, lo][:, c0 - lo:c1 - lo], op=MULT)
            for acc in accs:
                nc.tensor.matmul(out=acc[:, 0:w], lhsT=ident[:], rhs=t2[:], start=False, stop=True)
                nc.scalar.copy(out=o[:], in_=acc[:, 0:w])
                nc.scalar.dma_start(out=out[h * P:(h + 1) * P, lo:hi], in_=o[:])
            if not accs:
                for j in range(2):
                    js = slice(j * w // 2, (j + 1) * w // 2)
                    nc.vector.tensor_tensor(out=o[:, js], in0=t1[:, js], in1=t2[:, js], op=ADD)
                    nc.sync.dma_start(out=out[h * P:(h + 1) * P, lo + j * w // 2:lo + (j + 1) * w // 2], in_=o[:, js])

        combine(0, 0, T // 2, [banks[0, 0]])
        combine(0, T // 2, T, [banks[0, 1]])
        combine(1, 0, 384, [banks[0, 2]])
        combine(1, 384, T, [])
